import numpy as np
import ml_dtypes


def mxq(x, axis, fmt="e4m3"):
    dtype, down = {"e4m3": (ml_dtypes.float8_e4m3fn, 7), "e5m2": (ml_dtypes.float8_e5m2, 14)}[fmt]
    v = np.moveaxis(np.asarray(x, np.float32).astype(ml_dtypes.bfloat16).astype(np.float64), axis, -1)
    blocks = v.reshape(v.shape[:-1] + (-1, 32))
    amax = np.abs(blocks).max(-1, keepdims=True)
    byte = np.maximum(np.where(amax > 0, np.frexp(amax)[1] - 1 + 127, 0) - down, 1)
    scale = np.exp2(byte - 127.0)
    codes = (blocks / scale).astype(np.float32).astype(dtype).astype(np.float64)
    return np.moveaxis((codes * scale).reshape(v.shape), -1, axis)


WIDE = False


def mx_kscale(k):
    if not WIDE:
        return np.ones(k)
    levels = np.array([10, -10, 5, -5, 0])
    if k % 512:
        return np.exp2(np.random.permutation(np.resize(levels, k // 32))).repeat(32)
    a = np.empty((k // 512, 16))
    for p in range(k // 512):
        a[p, :8] = np.random.permutation(np.resize(levels, 8))
        for g in range(8):
            far = levels[np.abs(levels - a[p, g]) >= 10]
            a[p, g + 8] = far[np.random.randint(len(far))]
    return np.exp2(a.ravel()).repeat(32)


def f64(x):
    return np.asarray(x).astype(np.float64)


def striped(idx):
    return np.tile(idx.reshape(-1, 16).T, (8, 1)).astype(np.uint16)


def unstriped(offs):
    return offs[:16].T.reshape(-1).astype(np.int64)


E2M1 = np.array([0.0, 0.5, 1.0, 1.5, 2.0, 3.0, 4.0, 6.0, -0.0, -0.5, -1.0, -1.5, -2.0, -3.0, -4.0, -6.0])


def pack_weight(w, fmt):
    k, n = w.shape
    w = f64(np.asarray(w, np.float32).astype(ml_dtypes.bfloat16)).reshape(k // 32, 32, n)
    amax = np.abs(w).max(1)
    if fmt == "e4m3":
        byte = np.frexp(amax)[1] - 1 + 127 - 7
    else:
        mant, ex = np.frexp(amax / 6.0)
        byte = np.where(mant > 0.5, ex, ex - 1) + 127
    byte = np.clip(np.where(amax > 0, byte, 1), 1, 254)
    scaled = (w * np.exp2(127.0 - byte)[:, None, :]).reshape(k, n).astype(np.float32)
    by_word = np.ascontiguousarray(scaled.reshape(k // 512, 128, 4, n).transpose(0, 1, 3, 2))
    if fmt == "e4m3":
        words = by_word.astype(ml_dtypes.float8_e4m3fn).view(np.uint8)
    else:
        c = by_word.astype(ml_dtypes.float4_e2m1fn).view(np.uint8) & 0xF
        words = (c[..., 0::2] | (c[..., 1::2] << 4)).reshape(k // 512, 128, 2 * n)
    return np.ascontiguousarray(words), np.ascontiguousarray(byte.astype(np.uint8).reshape(k // 512, 16, n))


def unpack_weight(words, scales, fmt):
    g, _, n = scales.shape
    words = np.ascontiguousarray(words).reshape(g, 128, n, -1)
    if fmt == "e4m3":
        vals = words.view(ml_dtypes.float8_e4m3fn).astype(np.float64)
    else:
        nib = np.empty((g, 128, n, 4), np.uint8)
        nib[..., 0::2] = words & 0xF
        nib[..., 1::2] = words >> 4
        vals = E2M1[nib]
    vals = vals * np.repeat(np.exp2(scales.astype(np.float64) - 127.0), 8, axis=1)[..., None]
    return vals.transpose(0, 1, 3, 2).reshape(g * 512, n)


def relu(v):
    return np.maximum(v, 0.0)


K, T, E, H, N = 1024, 1536, 8, 512, 128
COUNTS = (128, 128, 128, 128, 128, 512, 128, 256)
STARTS = np.cumsum((0,) + COUNTS)


def by_expert(wq, xq):
    return np.concatenate([wq[e].T @ xq[:, STARTS[e]:STARTS[e + 1]] for e in range(E)], axis=1)


def setup_inputs():
    n = np.random.standard_normal
    s = mx_kscale(K)[:, None]
    u = mx_kscale(H)
    expert = np.random.permutation(np.repeat(np.arange(E), COUNTS))
    slot_token = np.argsort(expert, kind="stable")
    w1 = [pack_weight(m, "e2m1") for m in n((E, K, H)) / np.sqrt(K) / s[None] * u[None, None, :]]
    w2 = [pack_weight(m, "e2m1") for m in n((E, H, N)) / np.sqrt(H) / u[None, :, None]]
    return {
        "xT": (n((K, T)) * s).astype(np.float32),
        "w1_words": np.stack([m[0] for m in w1]),
        "w1_scales": np.stack([m[1] for m in w1]),
        "w2_words": np.stack([m[0] for m in w2]),
        "w2_scales": np.stack([m[1] for m in w2]),
        "gate": np.tile(np.random.uniform(0.2, 1.0, T), (N, 1)).astype(np.float32),
        "offs": striped(slot_token),
    }


def reference(xT, w1_words, w1_scales, w2_words, w2_scales, gate, offs):
    idx = unstriped(offs)
    w1 = np.stack([unpack_weight(w1_words[e], w1_scales[e], "e2m1") for e in range(E)])
    w2 = np.stack([unpack_weight(w2_words[e], w2_scales[e], "e2m1") for e in range(E)])
    xq = mxq(f64(xT)[:, idx], 0, "e4m3")
    h = relu(by_expert(w1, xq))
    y = by_expert(w2, mxq(h, 0, "e4m3"))
    out = np.zeros((N, T))
    out[:, idx] = f64(gate) * y
    return out

@@ -1,0 +1,202 @@
+from contextlib import ExitStack
+
+import concourse.mybir as mybir
+from concourse.masks import make_identity
+
+F32 = mybir.dt.float32
+BF16 = mybir.dt.bfloat16
+I32 = mybir.dt.int32
+U32 = mybir.dt.uint32
+U16 = mybir.dt.uint16
+U8 = mybir.dt.uint8
+FP8X4 = mybir.dt.float8_e4m3fn_x4
+FP4X4 = mybir.dt.float4_e2m1fn_x4
+COPY = mybir.ActivationFunctionType.Copy
+RELU = mybir.ActivationFunctionType.Relu
+MULT = mybir.AluOpType.mult
+
+K, T, E, H, N = 1024, 1536, 8, 512, 128
+P = 128
+PASSES = K // 512
+COUNTS = (128, 128, 128, 128, 128, 512, 128, 256)
+EXPERT_OF_BLOCK = tuple(e for e in range(E) for b in range(COUNTS[e] // P))
+BLOCKS = T // P
+
+FLOPS = 2 * T * (K * H + H * N)
+
+LOADS = (
+    ((0, 256, "s"),),
+    ((256, 256, "s"), (512, 256, "v")),
+    ((768, 256, "s"), (1024, 256, "v")),
+    ((1280, 128, "s"), (1408, 128, "v")),
+)
+LOADS1 = (
+    ((0, 512, "s"),),
+    ((512, 512, "s"),),
+    ((1024, 256, "s"), (1280, 256, "s")),
+)
+GATHER0 = 768
+GROUP = 256
+
+
+def tile_moe_rag_mlp_relu_kernel(
+    tc, xT, w1_words, w1_scales, w2_words, w2_scales, gate, offs, out
+):
+    nc = tc.nc
+    with ExitStack() as ctx:
+        hold = ctx.enter_context(tc.tile_pool(name="hold", bufs=1))
+        psum_h = ctx.enter_context(tc.psum_pool(name="psum_h", bufs=5))
+        psum_t = ctx.enter_context(tc.psum_pool(name="psum_t", bufs=2))
+        psum_y = ctx.enter_context(tc.psum_pool(name="psum_y", bufs=1))
+
+        offsets = hold.tile([P, T // 16], U16, name="offsets")
+        nc.sync.dma_start(offsets[:], offs)
+
+        x_words = []
+        x_scales = []
+        for s in range(PASSES):
+            words = hold.tile([P, T], U32, name=f"x_words{s}", align_bytes=64)
+            scales = hold.tile([P, T], U8, name=f"x_scales{s}", align_bytes=64)
+            nc.gpsimd.memset(scales[:], 0)
+            x_words.append(words)
+            x_scales.append(scales)
+        w1_planes = hold.tile([P, E * PASSES * H], U8, name="w1_planes", align_bytes=64)
+        w2_planes = hold.tile([P, E * N], U8, name="w2_planes", align_bytes=64)
+        nc.vector.memset(w1_planes[:].bitcast(I32), 0)
+        nc.vector.memset(w2_planes[:].bitcast(I32), 0)
+        identity = hold.tile([P, P], F32, name="identity")
+        make_identity(nc, identity[:])
+
+        raw = {}
+
+        def load(s, chunk):
+            first = chunk[0][0]
+            width = sum(c[1] for c in chunk)
+            tile = hold.tile([P, 4, width], F32, name=f"raw{s}_{first}")
+            nc.sync.dma_start(
+                tile[:], xT[512 * s : 512 * (s + 1), first : first + width].rearrange("(p j) t -> p j t", j=4)
+            )
+            raw[s, first] = tile
+
+        def quantise(s, chunk):
+            first = chunk[0][0]
+            for t0, width, engine in chunk:
+                grouped = hold.tile([P, width, 4], BF16, name=f"grouped{s}_{t0}", align_bytes=64)
+                dst = grouped[:].rearrange("p (c i) j -> p c j i", i=4)
+                part = raw[s, first][:, :, t0 - first : t0 - first + width].rearrange("p j (c i) -> p c j i", i=4)
+                if engine == "s":
+                    nc.scalar.activation(dst, part, COPY)
+                else:
+                    nc.vector.tensor_copy(dst, part)
+                nc.vector.quantize_mx(
+                    out=x_words[s][:, t0 : t0 + width].bitcast(FP8X4),
+                    scales=x_scales[s][:, t0 : t0 + width],
+                    in_=grouped[:].rearrange("p t j -> p (t j)"),
+                )
+
+        for chunk in LOADS:
+            load(0, chunk)
+        for chunk in LOADS1:
+            load(1, chunk)
+
+        for q in range(4):
+            nc.sync.dma_start(
+                w1_planes[32 * q : 32 * q + 4, :].bitcast(I32).rearrange("r (a i) -> r a i", a=E * PASSES),
+                w1_scales.bitcast(I32).rearrange("e s q i -> q (e s) i")[4 * q : 4 * q + 4],
+            )
+        for q in range(4):
+            nc.sync.dma_start(
+                w2_planes[32 * q : 32 * q + 4, :].bitcast(I32).rearrange("r (a i) -> r a i", a=E),
+                w2_scales.bitcast(I32).rearrange("e s q i -> q (e s) i")[4 * q : 4 * q + 4],
+            )
+        w1 = []
+        for e in range(E):
+            tile = hold.tile([P, PASSES, 2 * H], U8, name=f"w1_{e}", align_bytes=64)
+            nc.sync.dma_start(tile[:].bitcast(I32), w1_words[e].bitcast(I32).rearrange("s p n -> p s n"))
+            w1.append(tile)
+            if e == 0:
+                w2 = hold.tile([P, E, 2 * N], U8, name="w2", align_bytes=64)
+                nc.sync.dma_start(w2[:].bitcast(I32), w2_words.bitcast(I32).rearrange("e s p n -> p (e s) n"))
+        gates = hold.tile([P, T], F32, name="gates")
+        nc.sync.dma_start(gates[:], gate)
+
+        gathered_words = {}
+        gathered_scales = {}
+
+        def gather(s, first, count):
+            words = hold.tile([P, count], U32, name=f"slot_words{s}_{first}", align_bytes=64)
+            scales = hold.tile([P, count], U8, name=f"slot_scales{s}_{first}", align_bytes=64)
+            listed = offsets[:, first // 16 : (first + count) // 16]
+            nc.vector.tensor_copy(words[:], x_words[s][:].indirect(listed))
+            nc.vector.tensor_copy(scales[:], x_scales[s][:].indirect(listed))
+            for b in range(count // P):
+                gathered_words[s, first // P + b] = words[:, P * b : P * (b + 1)]
+                gathered_scales[s, first // P + b] = scales[:, P * b : P * (b + 1)]
+
+        for chunk in LOADS:
+            quantise(0, chunk)
+        for first in range(0, T, GATHER0):
+            gather(0, first, GATHER0)
+        for chunk in LOADS1:
+            quantise(1, chunk)
+
+        results = {}
+        per_group = GROUP // P
+        for g in range(T // GROUP):
+            gather(1, g * GROUP, GROUP)
+            turned = psum_t.tile([P, per_group, 2, P], F32, name="turned")
+            for i in range(per_group):
+                b = g * per_group + i
+                e = EXPERT_OF_BLOCK[b]
+                acc = psum_h.tile([P, H], F32, name="acc")
+                for s in range(PASSES):
+                    nc.tensor.matmul_mx(
+                        acc[:],
+                        lhsT=gathered_words[s, b].bitcast(FP8X4),
+                        lhsT_scale=gathered_scales[s, b],
+                        rhs=w1[e][:, s, :].bitcast(FP4X4),
+                        rhs_scale=w1_planes[:, (PASSES * e + s) * H : (PASSES * e + s + 1) * H],
+                        start=(s == 0),
+                        stop=(s == PASSES - 1),
+                    )
+                hidden = hold.tile([P, H], BF16, name=f"hidden{b}", align_bytes=64)
+                nc.scalar.activation(
+                    hidden[:].rearrange("p (u q e) -> p q u e", u=2, e=2), acc[:].rearrange("p (q u e) -> p q u e", u=2, e=2), RELU
+                )
+                pairs = hidden[:].bitcast(F32)
+                for u in range(2):
+                    nc.tensor.transpose(turned[:, i, u, :], pairs[:, P * u : P * (u + 1)], identity[:])
+            h_grouped = hold.tile([P, GROUP, 4], BF16, name=f"h_grouped{g}", align_bytes=64)
+            nc.scalar.copy(
+                h_grouped[:].rearrange("p t j -> p (t j)").bitcast(F32).rearrange("p (b r u) -> p b r u", u=2, r=P),
+                turned[:].rearrange("p b u r -> p b r u"),
+            )
+            h_words = hold.tile([P, GROUP], U32, name=f"h_words{g}", align_bytes=64)
+            h_scales = hold.tile([P, GROUP], U8, name=f"h_scales{g}", align_bytes=64)
+            nc.vector.quantize_mx(
+                out=h_words[:].bitcast(FP8X4), scales=h_scales[:], in_=h_grouped[:].rearrange("p t j -> p (t j)")
+            )
+            y = psum_y.tile([P, GROUP], F32, name="y")
+            for i in range(per_group):
+                e = EXPERT_OF_BLOCK[g * per_group + i]
+                cols = slice(P * i, P * (i + 1))
+                nc.tensor.matmul_mx(
+                    y[:, cols],
+                    lhsT=w2[:, e, :].bitcast(FP4X4),
+                    lhsT_scale=w2_planes[:, N * e : N * (e + 1)],
+                    rhs=h_words[:, cols].bitcast(FP8X4),
+                    rhs_scale=h_scales[:, cols],
+                    start=True,
+                    stop=True,
+                )
+            result = hold.tile([P, GROUP], F32, name=f"result{g}")
+            nc.scalar.copy(result[:], y[:])
+            results[g] = result
+
+        by_token = hold.tile([P, T], F32, name="by_token")
+        for g in range(T // GROUP):
+            listed = offsets[:, g * GROUP // 16 : (g + 1) * GROUP // 16]
+            nc.vector.tensor_tensor(
+                by_token[:].indirect(listed), results[g][:], gates[:, g * GROUP : (g + 1) * GROUP], MULT
+            )
+        nc.sync.dma_start(out, by_token[:])

@@ -20,23 +20,22 @@ P = 128
 PASSES = K // 512
 COUNTS = (128, 128, 128, 128, 128, 512, 128, 256)
 EXPERT_OF_BLOCK = tuple(e for e in range(E) for b in range(COUNTS[e] // P))
-BLOCKS = T // P
 
 FLOPS = 2 * T * (K * H + H * N)
 
 LOADS = (
-    ((0, 256, "s"),),
-    ((256, 256, "s"), (512, 256, "v")),
-    ((768, 256, "s"), (1024, 256, "v")),
-    ((1280, 128, "s"), (1408, 128, "v")),
+    (((0, 256, "s"),), ((256, 256, "s"), (512, 256, "v"),), ((768, 256, "s"), (1024, 256, "v"),), ((1280, 128, "s"), (1408, 128, "v"),),),
+    (((0, 512, "s"),), ((512, 512, "s"),), ((1024, 256, "s"), (1280, 256, "v"),),),
 )
-LOADS1 = (
-    ((0, 512, "s"),),
-    ((512, 512, "s"),),
-    ((1024, 256, "s"), (1280, 256, "s")),
+WEIGHT_LOADS = ("x00", "x01", "x02", "x03", "x10", "x11", "x12", "sc:567", "w5", "w7", "w6", "s2", "ww", "sc:01234", "w0", "w1", "w2", "w3", "w4", "gate")
+GATHERS = (
+    ((640, 896), (0, 640)),
+    ((640, 256), (896, 256), (1152, 384), (0, 640)),
 )
-GATHER0 = 768
-GROUP = 256
+UNITS = ((640, 256), (896, 256), (1152, 256), (1408, 128), (0, 256), (256, 256), (512, 128))
+SCATTERS = ((640, 256), (896, 256), (1152, 192), (1344, 192), (0, 256), (256, 192), (448, 192))
+VECTOR_RELU = (0,)
+VECTOR_TURNED = (0,)
 
 
 def tile_moe_rag_mlp_relu_kernel(
@@ -45,9 +44,9 @@ def tile_moe_rag_mlp_relu_kernel(
     nc = tc.nc
     with ExitStack() as ctx:
         hold = ctx.enter_context(tc.tile_pool(name="hold", bufs=1))
-        psum_h = ctx.enter_context(tc.psum_pool(name="psum_h", bufs=5))
+        psum_h = ctx.enter_context(tc.psum_pool(name="psum_h", bufs=4))
         psum_t = ctx.enter_context(tc.psum_pool(name="psum_t", bufs=2))
-        psum_y = ctx.enter_context(tc.psum_pool(name="psum_y", bufs=1))
+        psum_y = ctx.enter_context(tc.psum_pool(name="psum_y", bufs=2))
 
         offsets = hold.tile([P, T // 16], U16, name="offsets")
         nc.sync.dma_start(offsets[:], offs)
@@ -94,109 +93,156 @@ def tile_moe_rag_mlp_relu_kernel(
                     in_=grouped[:].rearrange("p t j -> p (t j)"),
                 )
 
-        for chunk in LOADS:
-            load(0, chunk)
-        for chunk in LOADS1:
-            load(1, chunk)
+        w1 = {}
+        w2 = hold.tile([P, E, 2 * N], U8, name="w2", align_bytes=64)
+        gates = hold.tile([P, T], F32, name="gates")
 
-        for q in range(4):
-            nc.sync.dma_start(
-                w1_planes[32 * q : 32 * q + 4, :].bitcast(I32).rearrange("r (a i) -> r a i", a=E * PASSES),
-                w1_scales.bitcast(I32).rearrange("e s q i -> q (e s) i")[4 * q : 4 * q + 4],
-            )
-        for q in range(4):
-            nc.sync.dma_start(
-                w2_planes[32 * q : 32 * q + 4, :].bitcast(I32).rearrange("r (a i) -> r a i", a=E),
-                w2_scales.bitcast(I32).rearrange("e s q i -> q (e s) i")[4 * q : 4 * q + 4],
-            )
-        w1 = []
-        for e in range(E):
+        def load_w1(e):
             tile = hold.tile([P, PASSES, 2 * H], U8, name=f"w1_{e}", align_bytes=64)
             nc.sync.dma_start(tile[:].bitcast(I32), w1_words[e].bitcast(I32).rearrange("s p n -> p s n"))
-            w1.append(tile)
-            if e == 0:
-                w2 = hold.tile([P, E, 2 * N], U8, name="w2", align_bytes=64)
-                nc.sync.dma_start(w2[:].bitcast(I32), w2_words.bitcast(I32).rearrange("e s p n -> p (e s) n"))
-        gates = hold.tile([P, T], F32, name="gates")
-        nc.sync.dma_start(gates[:], gate)
+            w1[e] = tile
 
-        gathered_words = {}
-        gathered_scales = {}
+        def load_w1_scales(first, count):
+            a, b = PASSES * first, PASSES * (first + count)
+            for q in range(4):
+                nc.sync.dma_start(
+                    w1_planes[32 * q : 32 * q + 4, a * H : b * H].bitcast(I32).rearrange("r (a i) -> r a i", a=b - a),
+                    w1_scales.bitcast(I32)[first : first + count].rearrange("e s q i -> q (e s) i")[4 * q : 4 * q + 4],
+                )
+
+        def load_w2_scales():
+            for q in range(4):
+                nc.sync.dma_start(
+                    w2_planes[32 * q : 32 * q + 4, :].bitcast(I32).rearrange("r (a i) -> r a i", a=E),
+                    w2_scales.bitcast(I32).rearrange("e s q i -> q (e s) i")[4 * q : 4 * q + 4],
+                )
+
+        for item in WEIGHT_LOADS:
+            if item.startswith("x"):
+                load(int(item[1]), LOADS[int(item[1])][int(item[2])])
+            elif item.startswith("sc:"):
+                load_w1_scales(int(item[3]), len(item) - 3)
+            elif item == "s2":
+                load_w2_scales()
+            elif item == "ww":
+                nc.sync.dma_start(w2[:].bitcast(I32), w2_words.bitcast(I32).rearrange("e s p n -> p (e s) n"))
+            elif item == "gate":
+                nc.sync.dma_start(gates[:], gate)
+            else:
+                load_w1(int(item[1]))
+
+        slot_words = {}
+        slot_scales = {}
+        gathered = set()
 
         def gather(s, first, count):
             words = hold.tile([P, count], U32, name=f"slot_words{s}_{first}", align_bytes=64)
             scales = hold.tile([P, count], U8, name=f"slot_scales{s}_{first}", align_bytes=64)
             listed = offsets[:, first // 16 : (first + count) // 16]
-            nc.vector.tensor_copy(words[:], x_words[s][:].indirect(listed))
-            nc.vector.tensor_copy(scales[:], x_scales[s][:].indirect(listed))
+            if s == 0:
+                nc.vector.tensor_copy(words[:], x_words[s][:].indirect(listed))
+                nc.vector.tensor_copy(scales[:], x_scales[s][:].indirect(listed))
+            else:
+                nc.vector.tensor_copy(scales[:], x_scales[s][:].indirect(listed))
+                nc.vector.tensor_copy(words[:], x_words[s][:].indirect(listed))
             for b in range(count // P):
-                gathered_words[s, first // P + b] = words[:, P * b : P * (b + 1)]
-                gathered_scales[s, first // P + b] = scales[:, P * b : P * (b + 1)]
+                slot_words[s, first // P + b] = words[:, P * b : P * (b + 1)]
+                slot_scales[s, first // P + b] = scales[:, P * b : P * (b + 1)]
 
-        for chunk in LOADS:
+        for chunk in LOADS[0]:
             quantise(0, chunk)
-        for first in range(0, T, GATHER0):
-            gather(0, first, GATHER0)
-        for chunk in LOADS1:
+        for first, count in GATHERS[0]:
+            gather(0, first, count)
+        for chunk in LOADS[1]:
             quantise(1, chunk)
 
-        results = {}
-        per_group = GROUP // P
-        for g in range(T // GROUP):
-            gather(1, g * GROUP, GROUP)
-            turned = psum_t.tile([P, per_group, 2, P], F32, name="turned")
-            for i in range(per_group):
-                b = g * per_group + i
+        hidden_pairs = {}
+        quantised = {}
+        result = hold.tile([P, T], F32, name="result")
+
+        def layer1(first, count):
+            for b in range(first // P, (first + count) // P):
+                for piece in GATHERS[1]:
+                    if piece[0] <= b * P < piece[0] + piece[1] and piece not in gathered:
+                        gathered.add(piece)
+                        gather(1, piece[0], piece[1])
                 e = EXPERT_OF_BLOCK[b]
                 acc = psum_h.tile([P, H], F32, name="acc")
                 for s in range(PASSES):
                     nc.tensor.matmul_mx(
                         acc[:],
-                        lhsT=gathered_words[s, b].bitcast(FP8X4),
-                        lhsT_scale=gathered_scales[s, b],
+                        lhsT=slot_words[s, b].bitcast(FP8X4),
+                        lhsT_scale=slot_scales[s, b],
                         rhs=w1[e][:, s, :].bitcast(FP4X4),
                         rhs_scale=w1_planes[:, (PASSES * e + s) * H : (PASSES * e + s + 1) * H],
                         start=(s == 0),
                         stop=(s == PASSES - 1),
                     )
                 hidden = hold.tile([P, H], BF16, name=f"hidden{b}", align_bytes=64)
-                nc.scalar.activation(
-                    hidden[:].rearrange("p (u q e) -> p q u e", u=2, e=2), acc[:].rearrange("p (q u e) -> p q u e", u=2, e=2), RELU
-                )
-                pairs = hidden[:].bitcast(F32)
+                dst = hidden[:].rearrange("p (u q e) -> p q u e", u=2, e=2)
+                src = acc[:].rearrange("p (q u e) -> p q u e", u=2, e=2)
+                if b in VECTOR_RELU:
+                    nc.vector.tensor_scalar_max(dst, src, 0.0)
+                else:
+                    nc.scalar.activation(dst, src, RELU)
+                hidden_pairs[b] = hidden[:].bitcast(F32)
+
+        def turn(index, first, count):
+            blocks = count // P
+            turned = psum_t.tile([P, 2, 2, P], F32, name="turned")
+            for i in range(blocks):
+                pairs = hidden_pairs[first // P + i]
                 for u in range(2):
                     nc.tensor.transpose(turned[:, i, u, :], pairs[:, P * u : P * (u + 1)], identity[:])
-            h_grouped = hold.tile([P, GROUP, 4], BF16, name=f"h_grouped{g}", align_bytes=64)
-            nc.scalar.copy(
-                h_grouped[:].rearrange("p t j -> p (t j)").bitcast(F32).rearrange("p (b r u) -> p b r u", u=2, r=P),
-                turned[:].rearrange("p b u r -> p b r u"),
-            )
-            h_words = hold.tile([P, GROUP], U32, name=f"h_words{g}", align_bytes=64)
-            h_scales = hold.tile([P, GROUP], U8, name=f"h_scales{g}", align_bytes=64)
-            nc.vector.quantize_mx(
-                out=h_words[:].bitcast(FP8X4), scales=h_scales[:], in_=h_grouped[:].rearrange("p t j -> p (t j)")
-            )
-            y = psum_y.tile([P, GROUP], F32, name="y")
-            for i in range(per_group):
-                e = EXPERT_OF_BLOCK[g * per_group + i]
+            grouped = hold.tile([P, count, 4], BF16, name=f"h_grouped{first}", align_bytes=64)
+            flat = grouped[:].rearrange("p t j -> p (t j)")
+            dst = flat.bitcast(F32).rearrange("p (b r u) -> p b r u", u=2, r=P)
+            src = turned[:, :blocks].rearrange("p b u r -> p b r u")
+            if index in VECTOR_TURNED:
+                nc.vector.tensor_copy(dst, src)
+            else:
+                nc.scalar.copy(dst, src)
+            words = hold.tile([P, count], U32, name=f"h_words{first}", align_bytes=64)
+            scales = hold.tile([P, count], U8, name=f"h_scales{first}", align_bytes=64)
+            nc.vector.quantize_mx(out=words[:].bitcast(FP8X4), scales=scales[:], in_=flat)
+            quantised[first] = (words, scales)
+
+        def layer2(first, count):
+            words, scales = quantised[first]
+            y = psum_y.tile([P, count], F32, name="y")
+            for i in range(count // P):
+                e = EXPERT_OF_BLOCK[first // P + i]
                 cols = slice(P * i, P * (i + 1))
                 nc.tensor.matmul_mx(
                     y[:, cols],
                     lhsT=w2[:, e, :].bitcast(FP4X4),
                     lhsT_scale=w2_planes[:, N * e : N * (e + 1)],
-                    rhs=h_words[:, cols].bitcast(FP8X4),
-                    rhs_scale=h_scales[:, cols],
+                    rhs=words[:, cols].bitcast(FP8X4),
+                    rhs_scale=scales[:, cols],
                     start=True,
                     stop=True,
                 )
-            result = hold.tile([P, GROUP], F32, name=f"result{g}")
-            nc.scalar.copy(result[:], y[:])
-            results[g] = result
+            nc.scalar.copy(result[:, first : first + count], y[:])
 
         by_token = hold.tile([P, T], F32, name="by_token")
-        for g in range(T // GROUP):
-            listed = offsets[:, g * GROUP // 16 : (g + 1) * GROUP // 16]
-            nc.vector.tensor_tensor(
-                by_token[:].indirect(listed), results[g][:], gates[:, g * GROUP : (g + 1) * GROUP], MULT
-            )
+        scattered = set()
+
+        def scatter(units_done):
+            for first, count in SCATTERS:
+                units = [i for i, u in enumerate(UNITS) if u[0] < first + count and u[0] + u[1] > first]
+                if max(units) < units_done and first not in scattered:
+                    scattered.add(first)
+                    listed = offsets[:, first // 16 : (first + count) // 16]
+                    cols = slice(first, first + count)
+                    nc.vector.tensor_tensor(by_token[:].indirect(listed), result[:, cols], gates[:, cols], MULT)
+
+        for step in range(len(UNITS) + 4):
+            if step < len(UNITS):
+                layer1(*UNITS[step])
+            if 0 <= step - 2 < len(UNITS):
+                turn(step - 2, *UNITS[step - 2])
+            if 0 <= step - 4 < len(UNITS):
+                layer2(*UNITS[step - 4])
+            if 0 <= step - 4:
+                scatter(step - 4 + 1)
         nc.sync.dma_start(out, by_token[:])

@@ -25,7 +25,7 @@ FLOPS = 2 * T * (K * H + H * N)
 
 LOADS = (
     (((0, 256, "s"),), ((256, 256, "s"), (512, 256, "v"),), ((768, 256, "s"), (1024, 256, "v"),), ((1280, 128, "s"), (1408, 128, "v"),),),
-    (((0, 512, "s"),), ((512, 512, "s"),), ((1024, 256, "s"), (1280, 256, "v"),),),
+    (((0, 512, "s"),), ((512, 512, "s"),), ((1024, 256, "s"), (1280, 256, "s"),),),
 )
 WEIGHT_LOADS = ("x00", "x01", "x02", "x03", "x10", "x11", "x12", "sc:567", "w5", "w7", "w6", "s2", "ww", "sc:01234", "w0", "w1", "w2", "w3", "w4", "gate")
 GATHERS = (
@@ -34,8 +34,11 @@ GATHERS = (
 )
 UNITS = ((640, 256), (896, 256), (1152, 256), (1408, 128), (0, 256), (256, 256), (512, 128))
 SCATTERS = ((640, 256), (896, 256), (1152, 192), (1344, 192), (0, 256), (256, 192), (448, 192))
-VECTOR_RELU = (0,)
-VECTOR_TURNED = (0,)
+RESULTS = ((640, 256), (896, 256), (1152, 384), (0, 256), (256, 384))
+RESULT_TAG = {640: "result_a", 896: "result_b", 1152: "result_c", 0: "result_d", 256: "result_e"}
+H_BEHIND = {0: 640, 256: 896, 512: 1152}
+VECTOR_RELU = ()
+VECTOR_TURNED = ()
 
 
 def tile_moe_rag_mlp_relu_kernel(
@@ -158,7 +161,7 @@ def tile_moe_rag_mlp_relu_kernel(
 
         hidden_pairs = {}
         quantised = {}
-        result = hold.tile([P, T], F32, name="result")
+        results = {}
 
         def layer1(first, count):
             for b in range(first // P, (first + count) // P):
@@ -194,7 +197,8 @@ def tile_moe_rag_mlp_relu_kernel(
                 pairs = hidden_pairs[first // P + i]
                 for u in range(2):
                     nc.tensor.transpose(turned[:, i, u, :], pairs[:, P * u : P * (u + 1)], identity[:])
-            grouped = hold.tile([P, count, 4], BF16, name=f"h_grouped{first}", align_bytes=64)
+            tag = RESULT_TAG[H_BEHIND[first]] if first in H_BEHIND else f"h_grouped{first}"
+            grouped = hold.tile([P, count, 4], BF16, name=f"h_grouped{first}", tag=tag, align_bytes=64)
             flat = grouped[:].rearrange("p t j -> p (t j)")
             dst = flat.bitcast(F32).rearrange("p (b r u) -> p b r u", u=2, r=P)
             src = turned[:, :blocks].rearrange("p b u r -> p b r u")
@@ -222,7 +226,12 @@ def tile_moe_rag_mlp_relu_kernel(
                     start=True,
                     stop=True,
                 )
-            nc.scalar.copy(result[:, first : first + count], y[:])
+            for r0, width in RESULTS:
+                if r0 <= first < r0 + width:
+                    if r0 not in results:
+                        tile = hold.tile([P, width], F32, name=f"result{r0}", tag=RESULT_TAG[r0], align_bytes=64)
+                        results[r0] = tile
+                    nc.scalar.copy(results[r0][:, first - r0 : first - r0 + count], y[:])
 
         by_token = hold.tile([P, T], F32, name="by_token")
         scattered = set()
@@ -233,8 +242,14 @@ def tile_moe_rag_mlp_relu_kernel(
                 if max(units) < units_done and first not in scattered:
                     scattered.add(first)
                     listed = offsets[:, first // 16 : (first + count) // 16]
-                    cols = slice(first, first + count)
-                    nc.vector.tensor_tensor(by_token[:].indirect(listed), result[:, cols], gates[:, cols], MULT)
+                    for r0, width in RESULTS:
+                        if r0 <= first < r0 + width:
+                            nc.vector.tensor_tensor(
+                                by_token[:].indirect(listed),
+                                results[r0][:, first - r0 : first - r0 + count],
+                                gates[:, first : first + count],
+                                MULT,
+                            )
 
         for step in range(len(UNITS) + 4):
             if step < len(UNITS):

@@ -23,22 +23,31 @@ EXPERT_OF_BLOCK = tuple(e for e in range(E) for b in range(COUNTS[e] // P))
 
 FLOPS = 2 * T * (K * H + H * N)
 
-LOADS = (
-    (((0, 256, "s"),), ((256, 256, "s"), (512, 256, "v"),), ((768, 256, "s"), (1024, 256, "v"),), ((1280, 128, "s"), (1408, 128, "v"),),),
-    (((0, 512, "s"),), ((512, 512, "s"),), ((1024, 256, "s"), (1280, 256, "s"),),),
+TOKEN_LOADS = (
+    (
+        ((0, 256, "scalar"),),
+        ((256, 256, "scalar"), (512, 256, "vector")),
+        ((768, 256, "scalar"), (1024, 256, "vector")),
+        ((1280, 128, "scalar"), (1408, 128, "vector")),
+    ),
+    (
+        ((0, 256, "scalar"),),
+        ((256, 512, "scalar"),),
+        ((768, 512, "scalar"),),
+        ((1280, 256, "vector"),),
+    ),
 )
-WEIGHT_LOADS = ("x00", "x01", "x02", "x03", "x10", "x11", "x12", "sc:567", "w5", "w7", "w6", "s2", "ww", "sc:01234", "w0", "w1", "w2", "w3", "w4", "gate")
+
 GATHERS = (
     ((640, 896), (0, 640)),
     ((640, 256), (896, 256), (1152, 384), (0, 640)),
 )
 UNITS = ((640, 256), (896, 256), (1152, 256), (1408, 128), (0, 256), (256, 256), (512, 128))
-SCATTERS = ((640, 256), (896, 256), (1152, 192), (1344, 192), (0, 256), (256, 192), (448, 192))
+TURN_LAG = 2
+LAYER2_LAG = 4
 RESULTS = ((640, 256), (896, 256), (1152, 384), (0, 256), (256, 384))
-RESULT_TAG = {640: "result_a", 896: "result_b", 1152: "result_c", 0: "result_d", 256: "result_e"}
-H_BEHIND = {0: 640, 256: 896, 512: 1152}
-VECTOR_RELU = ()
-VECTOR_TURNED = ()
+SCATTERS = ((640, 256), (896, 256), (1152, 192), (1344, 192), (0, 256), (256, 192), (448, 192))
+BYTES_OF_RESULT = {0: 640, 256: 896, 512: 1152}
 
 
 def tile_moe_rag_mlp_relu_kernel(
@@ -47,8 +56,8 @@ def tile_moe_rag_mlp_relu_kernel(
     nc = tc.nc
     with ExitStack() as ctx:
         hold = ctx.enter_context(tc.tile_pool(name="hold", bufs=1))
-        psum_h = ctx.enter_context(tc.psum_pool(name="psum_h", bufs=4))
-        psum_t = ctx.enter_context(tc.psum_pool(name="psum_t", bufs=2))
+        psum_sums = ctx.enter_context(tc.psum_pool(name="psum_sums", bufs=4))
+        psum_turned = ctx.enter_context(tc.psum_pool(name="psum_turned", bufs=2))
         psum_y = ctx.enter_context(tc.psum_pool(name="psum_y", bufs=2))
 
         offsets = hold.tile([P, T // 16], U16, name="offsets")
@@ -70,94 +79,84 @@ def tile_moe_rag_mlp_relu_kernel(
         make_identity(nc, identity[:])
 
         raw = {}
-
-        def load(s, chunk):
-            first = chunk[0][0]
-            width = sum(c[1] for c in chunk)
-            tile = hold.tile([P, 4, width], F32, name=f"raw{s}_{first}")
-            nc.sync.dma_start(
-                tile[:], xT[512 * s : 512 * (s + 1), first : first + width].rearrange("(p j) t -> p j t", j=4)
-            )
-            raw[s, first] = tile
-
-        def quantise(s, chunk):
-            first = chunk[0][0]
-            for t0, width, engine in chunk:
-                grouped = hold.tile([P, width, 4], BF16, name=f"grouped{s}_{t0}", align_bytes=64)
-                dst = grouped[:].rearrange("p (c i) j -> p c j i", i=4)
-                part = raw[s, first][:, :, t0 - first : t0 - first + width].rearrange("p j (c i) -> p c j i", i=4)
-                if engine == "s":
-                    nc.scalar.activation(dst, part, COPY)
-                else:
-                    nc.vector.tensor_copy(dst, part)
-                nc.vector.quantize_mx(
-                    out=x_words[s][:, t0 : t0 + width].bitcast(FP8X4),
-                    scales=x_scales[s][:, t0 : t0 + width],
-                    in_=grouped[:].rearrange("p t j -> p (t j)"),
-                )
-
         w1 = {}
         w2 = hold.tile([P, E, 2 * N], U8, name="w2", align_bytes=64)
         gates = hold.tile([P, T], F32, name="gates")
+
+        def load_tokens(s, casts):
+            first = casts[0][0]
+            width = sum(cast[1] for cast in casts)
+            tile = hold.tile([P, 4, width], F32, name=f"raw{s}_{first}")
+            rows = xT[512 * s : 512 * (s + 1), first : first + width]
+            nc.sync.dma_start(tile[:], rows.rearrange("(p j) t -> p j t", j=4))
+            raw[s, first] = tile
 
         def load_w1(e):
             tile = hold.tile([P, PASSES, 2 * H], U8, name=f"w1_{e}", align_bytes=64)
             nc.sync.dma_start(tile[:].bitcast(I32), w1_words[e].bitcast(I32).rearrange("s p n -> p s n"))
             w1[e] = tile
 
-        def load_w1_scales(first, count):
-            a, b = PASSES * first, PASSES * (first + count)
+        def load_scales(planes, source, width):
+            rows = source.bitcast(I32).rearrange("e s q i -> q (e s) i")
+            count = source.shape[0] * source.shape[1]
             for q in range(4):
                 nc.sync.dma_start(
-                    w1_planes[32 * q : 32 * q + 4, a * H : b * H].bitcast(I32).rearrange("r (a i) -> r a i", a=b - a),
-                    w1_scales.bitcast(I32)[first : first + count].rearrange("e s q i -> q (e s) i")[4 * q : 4 * q + 4],
+                    planes[32 * q : 32 * q + 4, :].bitcast(I32).rearrange("r (a i) -> r a i", a=count),
+                    rows[4 * q : 4 * q + 4],
                 )
 
-        def load_w2_scales():
-            for q in range(4):
-                nc.sync.dma_start(
-                    w2_planes[32 * q : 32 * q + 4, :].bitcast(I32).rearrange("r (a i) -> r a i", a=E),
-                    w2_scales.bitcast(I32).rearrange("e s q i -> q (e s) i")[4 * q : 4 * q + 4],
-                )
+        def w1_planes_of(first, count):
+            width = PASSES * H
+            return w1_planes[:, width * first : width * (first + count)]
 
-        for item in WEIGHT_LOADS:
-            if item.startswith("x"):
-                load(int(item[1]), LOADS[int(item[1])][int(item[2])])
-            elif item.startswith("sc:"):
-                load_w1_scales(int(item[3]), len(item) - 3)
-            elif item == "s2":
-                load_w2_scales()
-            elif item == "ww":
-                nc.sync.dma_start(w2[:].bitcast(I32), w2_words.bitcast(I32).rearrange("e s p n -> p (e s) n"))
-            elif item == "gate":
-                nc.sync.dma_start(gates[:], gate)
-            else:
-                load_w1(int(item[1]))
+        for s in range(PASSES):
+            for casts in TOKEN_LOADS[s]:
+                load_tokens(s, casts)
+        load_scales(w1_planes_of(5, 3), w1_scales[5:8], H)
+        for e in (5, 7, 6):
+            load_w1(e)
+        load_scales(w2_planes, w2_scales, N)
+        nc.sync.dma_start(w2[:].bitcast(I32), w2_words.bitcast(I32).rearrange("e s p n -> p (e s) n"))
+        load_scales(w1_planes_of(0, 5), w1_scales[0:5], H)
+        for e in range(5):
+            load_w1(e)
+        nc.sync.dma_start(gates[:], gate)
+
+        def quantise_tokens(s, casts):
+            first = casts[0][0]
+            for t0, tokens, engine in casts:
+                grouped = hold.tile([P, tokens, 4], BF16, name=f"grouped{s}_{t0}", align_bytes=64)
+                dst = grouped[:].rearrange("p (c i) j -> p c j i", i=4)
+                src = raw[s, first][:, :, t0 - first : t0 - first + tokens].rearrange("p j (c i) -> p c j i", i=4)
+                if engine == "scalar":
+                    nc.scalar.activation(dst, src, COPY)
+                else:
+                    nc.vector.tensor_copy(dst, src)
+                nc.vector.quantize_mx(
+                    out=x_words[s][:, t0 : t0 + tokens].bitcast(FP8X4),
+                    scales=x_scales[s][:, t0 : t0 + tokens],
+                    in_=grouped[:].rearrange("p t j -> p (t j)"),
+                )
 
         slot_words = {}
         slot_scales = {}
-        gathered = set()
 
         def gather(s, first, count):
             words = hold.tile([P, count], U32, name=f"slot_words{s}_{first}", align_bytes=64)
             scales = hold.tile([P, count], U8, name=f"slot_scales{s}_{first}", align_bytes=64)
             listed = offsets[:, first // 16 : (first + count) // 16]
-            if s == 0:
-                nc.vector.tensor_copy(words[:], x_words[s][:].indirect(listed))
-                nc.vector.tensor_copy(scales[:], x_scales[s][:].indirect(listed))
-            else:
-                nc.vector.tensor_copy(scales[:], x_scales[s][:].indirect(listed))
-                nc.vector.tensor_copy(words[:], x_words[s][:].indirect(listed))
+            nc.vector.tensor_copy(scales[:], x_scales[s][:].indirect(listed))
+            nc.vector.tensor_copy(words[:], x_words[s][:].indirect(listed))
             for b in range(count // P):
                 slot_words[s, first // P + b] = words[:, P * b : P * (b + 1)]
                 slot_scales[s, first // P + b] = scales[:, P * b : P * (b + 1)]
 
-        for chunk in LOADS[0]:
-            quantise(0, chunk)
+        for casts in TOKEN_LOADS[0]:
+            quantise_tokens(0, casts)
         for first, count in GATHERS[0]:
             gather(0, first, count)
-        for chunk in LOADS[1]:
-            quantise(1, chunk)
+        for casts in TOKEN_LOADS[1]:
+            quantise_tokens(1, casts)
 
         hidden_pairs = {}
         quantised = {}
@@ -166,46 +165,43 @@ def tile_moe_rag_mlp_relu_kernel(
         def layer1(first, count):
             for b in range(first // P, (first + count) // P):
                 for piece in GATHERS[1]:
-                    if piece[0] <= b * P < piece[0] + piece[1] and piece not in gathered:
-                        gathered.add(piece)
+                    if piece[0] == P * b:
                         gather(1, piece[0], piece[1])
                 e = EXPERT_OF_BLOCK[b]
-                acc = psum_h.tile([P, H], F32, name="acc")
+                sums = psum_sums.tile([P, H], F32, name="sums")
                 for s in range(PASSES):
+                    a = PASSES * e + s
                     nc.tensor.matmul_mx(
-                        acc[:],
+                        sums[:],
                         lhsT=slot_words[s, b].bitcast(FP8X4),
                         lhsT_scale=slot_scales[s, b],
                         rhs=w1[e][:, s, :].bitcast(FP4X4),
-                        rhs_scale=w1_planes[:, (PASSES * e + s) * H : (PASSES * e + s + 1) * H],
+                        rhs_scale=w1_planes[:, a * H : (a + 1) * H],
                         start=(s == 0),
                         stop=(s == PASSES - 1),
                     )
                 hidden = hold.tile([P, H], BF16, name=f"hidden{b}", align_bytes=64)
-                dst = hidden[:].rearrange("p (u q e) -> p q u e", u=2, e=2)
-                src = acc[:].rearrange("p (q u e) -> p q u e", u=2, e=2)
-                if b in VECTOR_RELU:
-                    nc.vector.tensor_scalar_max(dst, src, 0.0)
-                else:
-                    nc.scalar.activation(dst, src, RELU)
+                nc.scalar.activation(
+                    hidden[:].rearrange("p (u q r) -> p q u r", u=2, r=2),
+                    sums[:].rearrange("p (q u r) -> p q u r", u=2, r=2),
+                    RELU,
+                )
                 hidden_pairs[b] = hidden[:].bitcast(F32)
 
-        def turn(index, first, count):
+        def turn(first, count):
             blocks = count // P
-            turned = psum_t.tile([P, 2, 2, P], F32, name="turned")
+            turned = psum_turned.tile([P, 2, 2, P], F32, name="turned")
             for i in range(blocks):
                 pairs = hidden_pairs[first // P + i]
                 for u in range(2):
                     nc.tensor.transpose(turned[:, i, u, :], pairs[:, P * u : P * (u + 1)], identity[:])
-            tag = RESULT_TAG[H_BEHIND[first]] if first in H_BEHIND else f"h_grouped{first}"
+            tag = f"result{BYTES_OF_RESULT[first]}" if first in BYTES_OF_RESULT else f"h_grouped{first}"
             grouped = hold.tile([P, count, 4], BF16, name=f"h_grouped{first}", tag=tag, align_bytes=64)
             flat = grouped[:].rearrange("p t j -> p (t j)")
-            dst = flat.bitcast(F32).rearrange("p (b r u) -> p b r u", u=2, r=P)
-            src = turned[:, :blocks].rearrange("p b u r -> p b r u")
-            if index in VECTOR_TURNED:
-                nc.vector.tensor_copy(dst, src)
-            else:
-                nc.scalar.copy(dst, src)
+            nc.scalar.copy(
+                flat.bitcast(F32).rearrange("p (b t u) -> p b t u", u=2, t=P),
+                turned[:, :blocks].rearrange("p b u t -> p b t u"),
+            )
             words = hold.tile([P, count], U32, name=f"h_words{first}", align_bytes=64)
             scales = hold.tile([P, count], U8, name=f"h_scales{first}", align_bytes=64)
             nc.vector.quantize_mx(out=words[:].bitcast(FP8X4), scales=scales[:], in_=flat)
@@ -226,38 +222,36 @@ def tile_moe_rag_mlp_relu_kernel(
                     start=True,
                     stop=True,
                 )
-            for r0, width in RESULTS:
-                if r0 <= first < r0 + width:
+            for r0, slots in RESULTS:
+                if r0 <= first < r0 + slots:
                     if r0 not in results:
-                        tile = hold.tile([P, width], F32, name=f"result{r0}", tag=RESULT_TAG[r0], align_bytes=64)
+                        tile = hold.tile([P, slots], F32, name=f"result{r0}", tag=f"result{r0}", align_bytes=64)
                         results[r0] = tile
                     nc.scalar.copy(results[r0][:, first - r0 : first - r0 + count], y[:])
 
         by_token = hold.tile([P, T], F32, name="by_token")
         scattered = set()
 
-        def scatter(units_done):
+        def scatter_ready(units_done):
             for first, count in SCATTERS:
-                units = [i for i, u in enumerate(UNITS) if u[0] < first + count and u[0] + u[1] > first]
-                if max(units) < units_done and first not in scattered:
+                needs = [i for i, u in enumerate(UNITS) if u[0] < first + count and u[0] + u[1] > first]
+                if max(needs) < units_done and first not in scattered:
                     scattered.add(first)
-                    listed = offsets[:, first // 16 : (first + count) // 16]
-                    for r0, width in RESULTS:
-                        if r0 <= first < r0 + width:
+                    for r0, slots in RESULTS:
+                        if r0 <= first < r0 + slots:
                             nc.vector.tensor_tensor(
-                                by_token[:].indirect(listed),
+                                by_token[:].indirect(offsets[:, first // 16 : (first + count) // 16]),
                                 results[r0][:, first - r0 : first - r0 + count],
                                 gates[:, first : first + count],
                                 MULT,
                             )
 
-        for step in range(len(UNITS) + 4):
+        for step in range(len(UNITS) + LAYER2_LAG):
             if step < len(UNITS):
                 layer1(*UNITS[step])
-            if 0 <= step - 2 < len(UNITS):
-                turn(step - 2, *UNITS[step - 2])
-            if 0 <= step - 4 < len(UNITS):
-                layer2(*UNITS[step - 4])
-            if 0 <= step - 4:
-                scatter(step - 4 + 1)
+            if 0 <= step - TURN_LAG < len(UNITS):
+                turn(*UNITS[step - TURN_LAG])
+            if 0 <= step - LAYER2_LAG:
+                layer2(*UNITS[step - LAYER2_LAG])
+                scatter_ready(step - LAYER2_LAG + 1)
         nc.sync.dma_start(out, by_token[:])

from contextlib import ExitStack

import concourse.mybir as mybir
from concourse.masks import make_identity

F32 = mybir.dt.float32
BF16 = mybir.dt.bfloat16
I32 = mybir.dt.int32
U32 = mybir.dt.uint32
U16 = mybir.dt.uint16
U8 = mybir.dt.uint8
FP8X4 = mybir.dt.float8_e4m3fn_x4
FP4X4 = mybir.dt.float4_e2m1fn_x4
COPY = mybir.ActivationFunctionType.Copy
RELU = mybir.ActivationFunctionType.Relu
MULT = mybir.AluOpType.mult

K, T, E, H, N = 1024, 1536, 8, 512, 128
P = 128
PASSES = K // 512
COUNTS = (128, 128, 128, 128, 128, 512, 128, 256)
EXPERT_OF_BLOCK = tuple(e for e in range(E) for b in range(COUNTS[e] // P))

FLOPS = 2 * T * (K * H + H * N)

TOKEN_LOADS = (
    (
        ((0, 256, "scalar"),),
        ((256, 256, "scalar"), (512, 256, "vector")),
        ((768, 256, "scalar"), (1024, 256, "vector")),
        ((1280, 128, "scalar"), (1408, 128, "vector")),
    ),
    (
        ((0, 256, "scalar"),),
        ((256, 512, "scalar"),),
        ((768, 512, "scalar"),),
        ((1280, 256, "vector"),),
    ),
)

GATHERS = (
    ((640, 896), (0, 640)),
    ((640, 256), (896, 256), (1152, 384), (0, 640)),
)
UNITS = ((640, 256), (896, 256), (1152, 256), (1408, 128), (0, 256), (256, 256), (512, 128))
TURN_LAG = 2
LAYER2_LAG = 4
RESULTS = ((640, 256), (896, 256), (1152, 384), (0, 256), (256, 384))
SCATTERS = ((640, 256), (896, 256), (1152, 192), (1344, 192), (0, 256), (256, 192), (448, 192))
BYTES_OF_RESULT = {0: 640, 256: 896, 512: 1152}


def tile_moe_rag_mlp_relu_kernel(
    tc, xT, w1_words, w1_scales, w2_words, w2_scales, gate, offs, out
):
    nc = tc.nc
    with ExitStack() as ctx:
        hold = ctx.enter_context(tc.tile_pool(name="hold", bufs=1))
        psum_sums = ctx.enter_context(tc.psum_pool(name="psum_sums", bufs=4))
        psum_turned = ctx.enter_context(tc.psum_pool(name="psum_turned", bufs=2))
        psum_y = ctx.enter_context(tc.psum_pool(name="psum_y", bufs=2))

        offsets = hold.tile([P, T // 16], U16, name="offsets")
        nc.sync.dma_start(offsets[:], offs)

        x_words = []
        x_scales = []
        for s in range(PASSES):
            words = hold.tile([P, T], U32, name=f"x_words{s}", align_bytes=64)
            scales = hold.tile([P, T], U8, name=f"x_scales{s}", align_bytes=64)
            nc.gpsimd.memset(scales[:], 0)
            x_words.append(words)
            x_scales.append(scales)
        w1_planes = hold.tile([P, E * PASSES * H], U8, name="w1_planes", align_bytes=64)
        w2_planes = hold.tile([P, E * N], U8, name="w2_planes", align_bytes=64)
        nc.vector.memset(w1_planes[:].bitcast(I32), 0)
        nc.vector.memset(w2_planes[:].bitcast(I32), 0)
        identity = hold.tile([P, P], F32, name="identity")
        make_identity(nc, identity[:])

        raw = {}
        w1 = {}
        w2 = hold.tile([P, E, 2 * N], U8, name="w2", align_bytes=64)
        gates = hold.tile([P, T], F32, name="gates")

        def load_tokens(s, casts):
            first = casts[0][0]
            width = sum(cast[1] for cast in casts)
            tile = hold.tile([P, 4, width], F32, name=f"raw{s}_{first}")
            rows = xT[512 * s : 512 * (s + 1), first : first + width]
            nc.sync.dma_start(tile[:], rows.rearrange("(p j) t -> p j t", j=4))
            raw[s, first] = tile

        def load_w1(e):
            tile = hold.tile([P, PASSES, 2 * H], U8, name=f"w1_{e}", align_bytes=64)
            nc.sync.dma_start(tile[:].bitcast(I32), w1_words[e].bitcast(I32).rearrange("s p n -> p s n"))
            w1[e] = tile

        def load_scales(planes, source, width):
            rows = source.bitcast(I32).rearrange("e s q i -> q (e s) i")
            count = source.shape[0] * source.shape[1]
            for q in range(4):
                nc.sync.dma_start(
                    planes[32 * q : 32 * q + 4, :].bitcast(I32).rearrange("r (a i) -> r a i", a=count),
                    rows[4 * q : 4 * q + 4],
                )

        def w1_planes_of(first, count):
            width = PASSES * H
            return w1_planes[:, width * first : width * (first + count)]

        for s in range(PASSES):
            for casts in TOKEN_LOADS[s]:
                load_tokens(s, casts)
        load_scales(w1_planes_of(5, 3), w1_scales[5:8], H)
        for e in (5, 7, 6):
            load_w1(e)
        load_scales(w2_planes, w2_scales, N)
        nc.sync.dma_start(w2[:].bitcast(I32), w2_words.bitcast(I32).rearrange("e s p n -> p (e s) n"))
        load_scales(w1_planes_of(0, 5), w1_scales[0:5], H)
        for e in range(5):
            load_w1(e)
        nc.sync.dma_start(gates[:], gate)

        def quantise_tokens(s, casts):
            first = casts[0][0]
            for t0, tokens, engine in casts:
                grouped = hold.tile([P, tokens, 4], BF16, name=f"grouped{s}_{t0}", align_bytes=64)
                dst = grouped[:].rearrange("p (c i) j -> p c j i", i=4)
                src = raw[s, first][:, :, t0 - first : t0 - first + tokens].rearrange("p j (c i) -> p c j i", i=4)
                if engine == "scalar":
                    nc.scalar.activation(dst, src, COPY)
                else:
                    nc.vector.tensor_copy(dst, src)
                nc.vector.quantize_mx(
                    out=x_words[s][:, t0 : t0 + tokens].bitcast(FP8X4),
                    scales=x_scales[s][:, t0 : t0 + tokens],
                    in_=grouped[:].rearrange("p t j -> p (t j)"),
                )

        slot_words = {}
        slot_scales = {}

        def gather(s, first, count):
            words = hold.tile([P, count], U32, name=f"slot_words{s}_{first}", align_bytes=64)
            scales = hold.tile([P, count], U8, name=f"slot_scales{s}_{first}", align_bytes=64)
            listed = offsets[:, first // 16 : (first + count) // 16]
            nc.vector.tensor_copy(scales[:], x_scales[s][:].indirect(listed))
            nc.vector.tensor_copy(words[:], x_words[s][:].indirect(listed))
            for b in range(count // P):
                slot_words[s, first // P + b] = words[:, P * b : P * (b + 1)]
                slot_scales[s, first // P + b] = scales[:, P * b : P * (b + 1)]

        for casts in TOKEN_LOADS[0]:
            quantise_tokens(0, casts)
        for first, count in GATHERS[0]:
            gather(0, first, count)
        for casts in TOKEN_LOADS[1]:
            quantise_tokens(1, casts)

        hidden_pairs = {}
        quantised = {}
        results = {}

        def layer1(first, count):
            for b in range(first // P, (first + count) // P):
                for piece in GATHERS[1]:
                    if piece[0] == P * b:
                        gather(1, piece[0], piece[1])
                e = EXPERT_OF_BLOCK[b]
                sums = psum_sums.tile([P, H], F32, name="sums")
                for s in range(PASSES):
                    a = PASSES * e + s
                    nc.tensor.matmul_mx(
                        sums[:],
                        lhsT=slot_words[s, b].bitcast(FP8X4),
                        lhsT_scale=slot_scales[s, b],
                        rhs=w1[e][:, s, :].bitcast(FP4X4),
                        rhs_scale=w1_planes[:, a * H : (a + 1) * H],
                        start=(s == 0),
                        stop=(s == PASSES - 1),
                    )
                hidden = hold.tile([P, H], BF16, name=f"hidden{b}", align_bytes=64)
                nc.scalar.activation(
                    hidden[:].rearrange("p (u q r) -> p q u r", u=2, r=2),
                    sums[:].rearrange("p (q u r) -> p q u r", u=2, r=2),
                    RELU,
                )
                hidden_pairs[b] = hidden[:].bitcast(F32)

        def turn(first, count):
            blocks = count // P
            turned = psum_turned.tile([P, 2, 2, P], F32, name="turned")
            for i in range(blocks):
                pairs = hidden_pairs[first // P + i]
                for u in range(2):
                    nc.tensor.transpose(turned[:, i, u, :], pairs[:, P * u : P * (u + 1)], identity[:])
            tag = f"result{BYTES_OF_RESULT[first]}" if first in BYTES_OF_RESULT else f"h_grouped{first}"
            grouped = hold.tile([P, count, 4], BF16, name=f"h_grouped{first}", tag=tag, align_bytes=64)
            flat = grouped[:].rearrange("p t j -> p (t j)")
            nc.scalar.copy(
                flat.bitcast(F32).rearrange("p (b t u) -> p b t u", u=2, t=P),
                turned[:, :blocks].rearrange("p b u t -> p b t u"),
            )
            words = hold.tile([P, count], U32, name=f"h_words{first}", align_bytes=64)
            scales = hold.tile([P, count], U8, name=f"h_scales{first}", align_bytes=64)
            nc.vector.quantize_mx(out=words[:].bitcast(FP8X4), scales=scales[:], in_=flat)
            quantised[first] = (words, scales)

        def layer2(first, count):
            words, scales = quantised[first]
            y = psum_y.tile([P, count], F32, name="y")
            for i in range(count // P):
                e = EXPERT_OF_BLOCK[first // P + i]
                cols = slice(P * i, P * (i + 1))
                nc.tensor.matmul_mx(
                    y[:, cols],
                    lhsT=w2[:, e, :].bitcast(FP4X4),
                    lhsT_scale=w2_planes[:, N * e : N * (e + 1)],
                    rhs=words[:, cols].bitcast(FP8X4),
                    rhs_scale=scales[:, cols],
                    start=True,
                    stop=True,
                )
            for r0, slots in RESULTS:
                if r0 <= first < r0 + slots:
                    if r0 not in results:
                        tile = hold.tile([P, slots], F32, name=f"result{r0}", tag=f"result{r0}", align_bytes=64)
                        results[r0] = tile
                    nc.scalar.copy(results[r0][:, first - r0 : first - r0 + count], y[:])

        by_token = hold.tile([P, T], F32, name="by_token")
        scattered = set()

        def scatter_ready(units_done):
            for first, count in SCATTERS:
                needs = [i for i, u in enumerate(UNITS) if u[0] < first + count and u[0] + u[1] > first]
                if max(needs) < units_done and first not in scattered:
                    scattered.add(first)
                    for r0, slots in RESULTS:
                        if r0 <= first < r0 + slots:
                            nc.vector.tensor_tensor(
                                by_token[:].indirect(offsets[:, first // 16 : (first + count) // 16]),
                                results[r0][:, first - r0 : first - r0 + count],
                                gates[:, first : first + count],
                                MULT,
                            )

        for step in range(len(UNITS) + LAYER2_LAG):
            if step < len(UNITS):
                layer1(*UNITS[step])
            if 0 <= step - TURN_LAG < len(UNITS):
                turn(*UNITS[step - TURN_LAG])
            if 0 <= step - LAYER2_LAG:
                layer2(*UNITS[step - LAYER2_LAG])
                scatter_ready(step - LAYER2_LAG + 1)
        nc.sync.dma_start(out, by_token[:])
